import numpy as np
import ml_dtypes


def mxq(x, axis, fmt="e4m3"):
    dtype, down = {"e4m3": (ml_dtypes.float8_e4m3fn, 7), "e5m2": (ml_dtypes.float8_e5m2, 14)}[fmt]
    v = np.moveaxis(np.asarray(x, np.float32).astype(ml_dtypes.bfloat16).astype(np.float64), axis, -1)
    blocks = v.reshape(v.shape[:-1] + (-1, 32))
    amax = np.abs(blocks).max(-1, keepdims=True)
    byte = np.maximum(np.where(amax > 0, np.frexp(amax)[1] - 1 + 127, 0) - down, 1)
    scale = np.exp2(byte - 127.0)
    codes = (blocks / scale).astype(np.float32).astype(dtype).astype(np.float64)
    return np.moveaxis((codes * scale).reshape(v.shape), -1, axis)


WIDE = False


def mx_kscale(k):
    if not WIDE:
        return np.ones(k)
    levels = np.array([10, -10, 5, -5, 0])
    if k % 512:
        return np.exp2(np.random.permutation(np.resize(levels, k // 32))).repeat(32)
    a = np.empty((k // 512, 16))
    for p in range(k // 512):
        a[p, :8] = np.random.permutation(np.resize(levels, 8))
        for g in range(8):
            far = levels[np.abs(levels - a[p, g]) >= 10]
            a[p, g + 8] = far[np.random.randint(len(far))]
    return np.exp2(a.ravel()).repeat(32)


def f64(x):
    return np.asarray(x).astype(np.float64)


def striped(idx):
    return np.tile(np.asarray(idx).reshape(-1, 16).T, (8, 1)).astype(np.uint16)


def unstriped(offs):
    return offs[:16].T.reshape(-1).astype(np.int64)


E2M1 = np.array([0.0, 0.5, 1.0, 1.5, 2.0, 3.0, 4.0, 6.0, -0.0, -0.5, -1.0, -1.5, -2.0, -3.0, -4.0, -6.0])


def pack_weight(w, fmt):
    k, n = w.shape
    w = f64(np.asarray(w, np.float32).astype(ml_dtypes.bfloat16)).reshape(k // 32, 32, n)
    amax = np.abs(w).max(1)
    if fmt == "e4m3":
        byte = np.frexp(amax)[1] - 1 + 127 - 7
    else:
        mant, ex = np.frexp(amax / 6.0)
        byte = np.where(mant > 0.5, ex, ex - 1) + 127
    byte = np.clip(np.where(amax > 0, byte, 1), 1, 254)
    scaled = (w * np.exp2(127.0 - byte)[:, None, :]).reshape(k, n).astype(np.float32)
    by_word = np.ascontiguousarray(scaled.reshape(k // 512, 128, 4, n).transpose(0, 1, 3, 2))
    if fmt == "e4m3":
        words = by_word.astype(ml_dtypes.float8_e4m3fn).view(np.uint8)
    else:
        c = by_word.astype(ml_dtypes.float4_e2m1fn).view(np.uint8) & 0xF
        words = (c[..., 0::2] | (c[..., 1::2] << 4)).reshape(k // 512, 128, 2 * n)
    return np.ascontiguousarray(words), np.ascontiguousarray(byte.astype(np.uint8).reshape(k // 512, 16, n))


def unpack_weight(words, scales, fmt):
    g, _, n = scales.shape
    words = np.ascontiguousarray(words).reshape(g, 128, n, -1)
    if fmt == "e4m3":
        vals = words.view(ml_dtypes.float8_e4m3fn).astype(np.float64)
    else:
        nib = np.empty((g, 128, n, 4), np.uint8)
        nib[..., 0::2] = words & 0xF
        nib[..., 1::2] = words >> 4
        vals = E2M1[nib]
    vals = vals * np.repeat(np.exp2(scales.astype(np.float64) - 127.0), 8, axis=1)[..., None]
    return vals.transpose(0, 1, 3, 2).reshape(g * 512, n)


def sigmoid(v):
    return 1.0 / (1.0 + np.exp(-v))


def bf(x):
    return np.asarray(x, np.float32).astype(ml_dtypes.bfloat16)


def planes(Y):
    r, m = Y.shape
    b = f64(bf(Y)).reshape(r // 32, 32, m)
    amax = np.abs(b).max(1)
    byte = np.clip(np.where(amax > 0, np.frexp(amax)[1] - 1 + 127 - 7, 1), 1, 254)
    codes = (b * np.exp2(127.0 - byte)[:, None, :]).reshape(r, m).astype(np.float32).astype(ml_dtypes.float8_e4m3fn).view(np.uint8)
    words = codes.reshape(r // 512, 128, 4, m).transpose(0, 1, 3, 2)
    return np.ascontiguousarray(words), np.ascontiguousarray(byte.astype(np.uint8).reshape(r // 512, 16, m))


D, T, I, Q, G, E = 512, 2048, 512, 256, 32, 512


def setup_inputs():
    n = np.random.standard_normal
    idx = np.random.permutation(T)[:I]
    fd = mx_kscale(D)
    fi = mx_kscale(I)
    ti = np.ones(T)
    ti[idx] = fi
    keysp = pack_weight(n((D, T)) / fd[:, None], "e2m1")
    return {
        "query": (n((D, Q)) * 1.0 / np.sqrt(D) * fd[:, None]).astype(np.float32),
        "keys_words": keysp[0],
        "keys_scales": keysp[1],
        "steep": (np.random.uniform(1.0, 4.0, (I, 1))).astype(np.float32),
        "us": (np.random.uniform(0.02, 0.1, (I, 1)) * fi[:, None]).astype(np.float32),
        "vals": (n((E, T)) / ti).astype(np.float32),
        "offs": striped(idx),
    }


def reference(query, keys_words, keys_scales, steep, us, vals, offs):
    idx = unstriped(offs)
    keysu = unpack_weight(keys_words, keys_scales, "e2m1")
    keysidxg = keysu[:, idx]
    queryq = mxq(f64(query), 0, "e4m3")
    a = keysidxg.T @ queryq
    b = a.reshape(I, G, Q // G).mean(axis=2)
    br = np.repeat(b, Q // G, axis=1)
    w = sigmoid((a - br) * f64(steep)) * f64(us)
    vt = f64(vals)[:, idx].T
    vtq = mxq(vt, 0, "e4m3")
    wq = mxq(w, 0, "e4m3")
    o = vtq.T @ wq
    words, scales = planes(o)
    return o, words, scales

@@ -1,0 +1,178 @@
+from contextlib import ExitStack
+
+import concourse.mybir as mybir
+from concourse.masks import make_identity
+
+D, T, I, Q, TEAM, E = 512, 2048, 512, 256, 8, 512
+FLOPS = 2 * D * I * Q + 2 * I * E * Q
+
+F32 = mybir.dt.float32
+BF16 = mybir.dt.bfloat16
+I32 = mybir.dt.int32
+U32 = mybir.dt.uint32
+U16 = mybir.dt.uint16
+U8 = mybir.dt.uint8
+FP8X4 = mybir.dt.float8_e4m3fn_x4
+FP4X4 = mybir.dt.float4_e2m1fn_x4
+ACT = mybir.ActivationFunctionType
+ALU = mybir.AluOpType
+
+P = 128
+PACK = 4
+HALF = Q // 2
+
+
+def tile_attend_teamcontrast_pl_kernel(tc, query, keys_words, keys_scales, steep, us, vals, offs, out_0, out_1, out_2):
+    nc = tc.nc
+    with ExitStack() as ctx:
+        sb = ctx.enter_context(tc.tile_pool(name="sb", bufs=1))
+        ps = ctx.enter_context(tc.psum_pool(name="ps", bufs=1))
+
+        offsets = sb.tile([P, I // 16], U16, name="offsets")
+        key_pool = sb.tile([P, T], U16, name="key_pool", align_bytes=64)
+        key_scale_pool = sb.tile([P, T], U8, name="key_scale_pool", align_bytes=64)
+        query_raw = sb.tile([P, PACK, Q], F32, name="query_raw")
+        steep_sb = sb.tile([P, PACK], F32, name="steep_sb")
+        us_sb = sb.tile([P, PACK], F32, name="us_sb")
+        val_pool = [sb.tile([P, T], F32, name="val_pool%d" % t) for t in range(PACK)]
+        identity = sb.tile([P, P], F32, name="identity")
+
+        nc.gpsimd.memset(key_scale_pool[:].bitcast(I32), 0)
+        nc.sync.dma_start(offsets[:], offs)
+        for quad in range(4):
+            nc.sync.dma_start(
+                key_scale_pool[32 * quad : 32 * quad + 4, :].bitcast(I32),
+                keys_scales[0, 4 * quad : 4 * quad + 4, :].bitcast(I32),
+            )
+        nc.sync.dma_start(key_pool[:].bitcast(I32), keys_words[0].bitcast(I32))
+        nc.sync.dma_start(query_raw[:], query.rearrange("(p j) q -> p j q", j=PACK))
+        vals_planes = vals.rearrange("(p t) n -> t p n", t=PACK)
+        for t in range(PACK):
+            nc.sync.dma_start(val_pool[t][:], vals_planes[t])
+            if t == 0:
+                nc.sync.dma_start(steep_sb[:], steep.rearrange("(p r) o -> p (r o)", r=PACK))
+                nc.sync.dma_start(us_sb[:], us.rearrange("(p r) o -> p (r o)", r=PACK))
+        make_identity(nc, identity[:])
+
+        key_listed = sb.tile([P, I], U16, name="key_listed")
+        key_scale_listed = sb.tile([P, I], U8, name="key_scale_listed")
+        nc.vector.tensor_copy(key_scale_listed[:], key_scale_pool[:].indirect(offsets[:]))
+        nc.vector.tensor_copy(key_listed[:], key_pool[:].indirect(offsets[:]))
+        key_dealt = sb.tile([P, PACK, P], U16, name="key_dealt", align_bytes=64)
+        key_scale_dealt = sb.tile([P, PACK, P], U8, name="key_scale_dealt", align_bytes=64)
+        nc.vector.tensor_copy(key_scale_dealt[:], key_scale_listed[:].rearrange("p (s r) -> p r s", r=PACK))
+        nc.vector.tensor_copy(key_dealt[:], key_listed[:].rearrange("p (s r) -> p r s", r=PACK))
+
+        query_grouped = sb.tile([P, Q, PACK], BF16, name="query_grouped", align_bytes=64)
+        nc.scalar.copy(
+            query_grouped[:].rearrange("p (c i) j -> p c j i", i=4),
+            query_raw[:].rearrange("p j (c i) -> p c j i", i=4),
+        )
+        query_codes = sb.tile([P, Q], U32, name="query_codes", align_bytes=64)
+        query_scales = sb.tile([P, Q], U8, name="query_scales", align_bytes=64)
+        nc.vector.quantize_mx(
+            out=query_codes[:].bitcast(FP8X4), scales=query_scales[:], in_=query_grouped[:].rearrange("p q j -> p (q j)")
+        )
+
+        weight_rows = sb.tile([P, PACK, Q], BF16, name="weight_rows")
+        for b in range(2):
+            scores = ps.tile([P, 2, Q], F32, name="scores%d" % b)
+            for rr in range(2):
+                r = 2 * b + rr
+                nc.tensor.matmul_mx(
+                    out=scores[:, rr, :],
+                    lhsT=key_dealt[:, r, :].bitcast(FP4X4),
+                    lhsT_scale=key_scale_dealt[:, r, :],
+                    rhs=query_codes[:].bitcast(FP8X4),
+                    rhs_scale=query_scales[:],
+                    start=True,
+                    stop=True,
+                )
+            teams = 2 * Q // TEAM
+            by_team = scores[:].rearrange("p r (g m) -> p (r g) m", m=TEAM)
+            team_sum = sb.tile([P, teams], F32, name="team_sum%d" % b)
+            nc.vector.tensor_reduce(out=team_sum[:], in_=by_team, axis=mybir.AxisListType.X, op=ALU.add)
+            contrast = sb.tile([P, 2, Q], F32, name="contrast%d" % b)
+            nc.vector.scalar_tensor_tensor(
+                out=contrast[:].rearrange("p r (g m) -> p (r g) m", m=TEAM),
+                in0=team_sum[:].unsqueeze(2).to_broadcast([P, teams, TEAM]),
+                scalar=-1.0 / TEAM,
+                in1=by_team,
+                op0=ALU.mult,
+                op1=ALU.add,
+            )
+            gate = sb.tile([P, 2, Q], F32, name="gate%d" % b)
+            for rr in range(2):
+                r = 2 * b + rr
+                nc.scalar.activation(gate[:, rr, :], contrast[:, rr, :], ACT.Sigmoid, scale=steep_sb[:, r : r + 1])
+            for rr in range(2):
+                r = 2 * b + rr
+                nc.scalar.activation(weight_rows[:, r, :], gate[:, rr, :], ACT.Copy, scale=us_sb[:, r : r + 1])
+        weight_grouped = sb.tile([P, Q, PACK], BF16, name="weight_grouped", align_bytes=64)
+        nc.scalar.copy(
+            weight_grouped[:].rearrange("p (c i) r -> p c r i", i=4),
+            weight_rows[:].rearrange("p r (c i) -> p c r i", i=4),
+        )
+        weight_codes = sb.tile([P, Q], U32, name="weight_codes", align_bytes=64)
+        weight_scales = sb.tile([P, Q], U8, name="weight_scales", align_bytes=64)
+        nc.vector.quantize_mx(
+            out=weight_codes[:].bitcast(FP8X4), scales=weight_scales[:], in_=weight_grouped[:].rearrange("p q r -> p (q r)")
+        )
+
+        result = [ps.tile([P, PACK, HALF], F32, name="result%d" % h) for h in range(2)]
+        out_rows = out_0.rearrange("(p t) q -> p t q", t=PACK)
+        result_sb = [sb.tile([P, Q], F32, name="result_sb%d" % t) for t in range(PACK)]
+        for t in range(PACK):
+            val_listed = sb.tile([P, I], BF16, name="val_listed%d" % t)
+            nc.vector.tensor_copy(val_listed[:], val_pool[t][:].indirect(offsets[:]))
+            pairs = val_listed[:].bitcast(F32)
+            turned = ps.tile([P, 2, P], F32, name="turned%d" % t)
+            for u in range(2):
+                nc.tensor.transpose(turned[:, u, :], pairs[:, u : I // 2 : 2], identity[:])
+            val_grouped = sb.tile([P, P, PACK], BF16, name="val_grouped%d" % t, align_bytes=64)
+            nc.scalar.copy(val_grouped[:].bitcast(F32), turned[:].rearrange("p u c -> p c u"))
+            val_codes = sb.tile([P, P], U32, name="val_codes%d" % t, align_bytes=64)
+            val_scales = sb.tile([P, P], U8, name="val_scales%d" % t, align_bytes=64)
+            nc.vector.quantize_mx(
+                out=val_codes[:].bitcast(FP8X4), scales=val_scales[:], in_=val_grouped[:].rearrange("p c r -> p (c r)")
+            )
+            for h in range(2):
+                cols = slice(h * HALF, (h + 1) * HALF)
+                nc.tensor.matmul_mx(
+                    out=result[h][:, t, :],
+                    lhsT=val_codes[:].bitcast(FP8X4),
+                    lhsT_scale=val_scales[:],
+                    rhs=weight_codes[:, cols].bitcast(FP8X4),
+                    rhs_scale=weight_scales[:, cols],
+                    start=True,
+                    stop=True,
+                )
+            if t < PACK - 1:
+                for h in range(2):
+                    nc.scalar.copy(result_sb[t][:, h * HALF : (h + 1) * HALF], result[h][:, t, :])
+                nc.sync.dma_start(out_rows[:, t, :], result_sb[t][:])
+
+        result_grouped = [sb.tile([P, HALF, PACK], BF16, name="result_grouped%d" % h, align_bytes=64) for h in range(2)]
+        nc.vector.tensor_copy(result_grouped[0][:], result[0][:].rearrange("p t q -> p q t"))
+        nc.scalar.copy(result_grouped[1][:], result[1][:].rearrange("p t q -> p q t"))
+        last = PACK - 1
+        for h in (1, 0):
+            nc.scalar.copy(result_sb[last][:, h * HALF : (h + 1) * HALF], result[h][:, last, :])
+        nc.scalar.dma_start(out_rows[:, last, :], result_sb[last][:])
+
+        result_codes = sb.tile([P, Q], U32, name="result_codes", align_bytes=64)
+        result_scales = sb.tile([P, Q], U8, name="result_scales", align_bytes=64)
+        for h in range(2):
+            cols = slice(h * HALF, (h + 1) * HALF)
+            nc.vector.quantize_mx(
+                out=result_codes[:, cols].bitcast(FP8X4),
+                scales=result_scales[:, cols],
+                in_=result_grouped[h][:].rearrange("p q t -> p (q t)"),
+            )
+        nc.sync.dma_start(out_1[0].rearrange("p q t -> p (q t)").bitcast(I32), result_codes[:].bitcast(I32))
+        for quad in range(4):
+            queue = nc.sync if quad < 2 else nc.scalar
+            queue.dma_start(
+                out_2[0, 4 * quad : 4 * quad + 4, :].bitcast(I32),
+                result_scales[32 * quad : 32 * quad + 4, :].bitcast(I32),
+            )

@@ -29,39 +29,50 @@ def tile_attend_teamcontrast_pl_kernel(tc, query, keys_words, keys_scales, steep
         ps = ctx.enter_context(tc.psum_pool(name="ps", bufs=1))
 
         offsets = sb.tile([P, I // 16], U16, name="offsets")
-        key_pool = sb.tile([P, T], U16, name="key_pool", align_bytes=64)
-        key_scale_pool = sb.tile([P, T], U8, name="key_scale_pool", align_bytes=64)
-        query_raw = sb.tile([P, PACK, Q], F32, name="query_raw")
-        steep_sb = sb.tile([P, PACK], F32, name="steep_sb")
+        key_pool = sb.tile([P, T], U16, name="key_pool", tag="plane1")
+        key_scale_pool = sb.tile([P, T], U8, name="key_scale_pool", tag="plane2")
+        query_raw = sb.tile([P, PACK, Q], F32, name="query_raw", tag="plane3", align_bytes=64)
+        steep_sb = sb.tile([P, PACK], F32, name="steep_sb", tag="plane0")
         us_sb = sb.tile([P, PACK], F32, name="us_sb")
-        val_pool = [sb.tile([P, T], F32, name="val_pool%d" % t) for t in range(PACK)]
         identity = sb.tile([P, P], F32, name="identity")
-
-        nc.gpsimd.memset(key_scale_pool[:].bitcast(I32), 0)
+        warmup_in = sb.tile([P, 1], F32, name="warmup_in")
+        warmup_out = sb.tile([P, 1], F32, name="warmup_out")
+        nc.vector.memset(key_scale_pool[:].bitcast(I32), 0)
+        nc.vector.memset(warmup_in[:], 0.0)
+        nc.scalar.activation(warmup_out[:], warmup_in[:], ACT.Sigmoid)
+        make_identity(nc, identity[:])
         nc.sync.dma_start(offsets[:], offs)
+        nc.sync.dma_start(steep_sb[:], steep.rearrange("(p r) o -> p (r o)", r=PACK))
+        nc.gpsimd.dma_start(us_sb[:], us.rearrange("(p r) o -> p (r o)", r=PACK))
+        nc.sync.dma_start(key_pool[:].bitcast(I32), keys_words[0].bitcast(I32))
+        nc.sync.dma_start(query_raw[:], query.rearrange("(p j) q -> p j q", j=PACK))
         for quad in range(4):
             nc.sync.dma_start(
                 key_scale_pool[32 * quad : 32 * quad + 4, :].bitcast(I32),
                 keys_scales[0, 4 * quad : 4 * quad + 4, :].bitcast(I32),
             )
-        nc.sync.dma_start(key_pool[:].bitcast(I32), keys_words[0].bitcast(I32))
-        nc.sync.dma_start(query_raw[:], query.rearrange("(p j) q -> p j q", j=PACK))
+        steep_per_member = sb.tile([P, PACK], F32, name="steep_per_member")
+        nc.vector.tensor_scalar(out=steep_per_member[:], in0=steep_sb[:], scalar1=1.0 / TEAM, scalar2=None, op0=ALU.mult)
         vals_planes = vals.rearrange("(p t) n -> t p n", t=PACK)
-        for t in range(PACK):
-            nc.sync.dma_start(val_pool[t][:], vals_planes[t])
-            if t == 0:
-                nc.sync.dma_start(steep_sb[:], steep.rearrange("(p r) o -> p (r o)", r=PACK))
-                nc.sync.dma_start(us_sb[:], us.rearrange("(p r) o -> p (r o)", r=PACK))
-        make_identity(nc, identity[:])
+
+        def load_values(t):
+            if t == PACK - 1:
+                plane = sb.tile([P, T], F32, name="val_pool%d" % t, tag="plane%d" % t, align_bytes=64)
+            else:
+                plane = sb.tile([P, T], F32, name="val_pool%d" % t, tag="plane%d" % t)
+            nc.sync.dma_start(plane[:], vals_planes[t])
+            return plane
+
+        val_pool = [load_values(t) for t in range(PACK)]
 
         key_listed = sb.tile([P, I], U16, name="key_listed")
         key_scale_listed = sb.tile([P, I], U8, name="key_scale_listed")
-        nc.vector.tensor_copy(key_scale_listed[:], key_scale_pool[:].indirect(offsets[:]))
         nc.vector.tensor_copy(key_listed[:], key_pool[:].indirect(offsets[:]))
+        nc.vector.tensor_copy(key_scale_listed[:], key_scale_pool[:].indirect(offsets[:]))
         key_dealt = sb.tile([P, PACK, P], U16, name="key_dealt", align_bytes=64)
         key_scale_dealt = sb.tile([P, PACK, P], U8, name="key_scale_dealt", align_bytes=64)
-        nc.vector.tensor_copy(key_scale_dealt[:], key_scale_listed[:].rearrange("p (s r) -> p r s", r=PACK))
         nc.vector.tensor_copy(key_dealt[:], key_listed[:].rearrange("p (s r) -> p r s", r=PACK))
+        nc.vector.tensor_copy(key_scale_dealt[:], key_scale_listed[:].rearrange("p (s r) -> p r s", r=PACK))
 
         query_grouped = sb.tile([P, Q, PACK], BF16, name="query_grouped", align_bytes=64)
         nc.scalar.copy(
@@ -74,101 +85,105 @@ def tile_attend_teamcontrast_pl_kernel(tc, query, keys_words, keys_scales, steep
             out=query_codes[:].bitcast(FP8X4), scales=query_scales[:], in_=query_grouped[:].rearrange("p q j -> p (q j)")
         )
 
-        weight_rows = sb.tile([P, PACK, Q], BF16, name="weight_rows")
-        for b in range(2):
-            scores = ps.tile([P, 2, Q], F32, name="scores%d" % b)
-            for rr in range(2):
-                r = 2 * b + rr
-                nc.tensor.matmul_mx(
-                    out=scores[:, rr, :],
-                    lhsT=key_dealt[:, r, :].bitcast(FP4X4),
-                    lhsT_scale=key_scale_dealt[:, r, :],
-                    rhs=query_codes[:].bitcast(FP8X4),
-                    rhs_scale=query_scales[:],
-                    start=True,
-                    stop=True,
-                )
-            teams = 2 * Q // TEAM
-            by_team = scores[:].rearrange("p r (g m) -> p (r g) m", m=TEAM)
-            team_sum = sb.tile([P, teams], F32, name="team_sum%d" % b)
-            nc.vector.tensor_reduce(out=team_sum[:], in_=by_team, axis=mybir.AxisListType.X, op=ALU.add)
-            contrast = sb.tile([P, 2, Q], F32, name="contrast%d" % b)
-            nc.vector.scalar_tensor_tensor(
-                out=contrast[:].rearrange("p r (g m) -> p (r g) m", m=TEAM),
-                in0=team_sum[:].unsqueeze(2).to_broadcast([P, teams, TEAM]),
-                scalar=-1.0 / TEAM,
-                in1=by_team,
-                op0=ALU.mult,
-                op1=ALU.add,
+        last = PACK - 1
+        late_listed = sb.tile([P, last * I], BF16, name="late_listed", tag="plane0")
+        late_grouped = sb.tile([P, last * I], BF16, name="late_grouped", align_bytes=64)
+        weight_rows = late_grouped[:, Q : Q + PACK * Q].rearrange("p (r q) -> p r q", r=PACK)
+        teams = 2 * Q // TEAM
+        scores = [ps.tile([P, 2, Q], F32, name="scores%d" % b, tag="scores%d" % b) for b in range(2)]
+        for r in range(PACK):
+            nc.tensor.matmul_mx(
+                out=scores[r // 2][:, r % 2, :],
+                lhsT=key_dealt[:, r, :].bitcast(FP4X4),
+                lhsT_scale=key_scale_dealt[:, r, :],
+                rhs=query_codes[:].bitcast(FP8X4),
+                rhs_scale=query_scales[:],
+                start=True,
+                stop=True,
             )
+        by_team = [scores[b][:].rearrange("p r (g m) -> p (r g) m", m=TEAM) for b in range(2)]
+        team_sum = [late_listed[:, : 2 * teams].bitcast(F32), late_listed[:, I - teams : I + teams].bitcast(F32)]
+        contrast = [sb.tile([P, 2, Q], F32, name="contrast%d" % b) for b in range(2)]
+        for b in range(2):
+            nc.vector.tensor_reduce(out=team_sum[b], in_=by_team[b], axis=mybir.AxisListType.X, op=ALU.add)
+        for b in range(2):
+            nc.vector.scalar_tensor_tensor(
+                out=contrast[b][:].rearrange("p r (g m) -> p (r g) m", m=TEAM),
+                in0=by_team[b],
+                scalar=float(TEAM),
+                in1=team_sum[b].unsqueeze(2).to_broadcast([P, teams, TEAM]),
+                op0=ALU.mult,
+                op1=ALU.subtract,
+            )
+        for b in range(2):
             gate = sb.tile([P, 2, Q], F32, name="gate%d" % b)
             for rr in range(2):
                 r = 2 * b + rr
-                nc.scalar.activation(gate[:, rr, :], contrast[:, rr, :], ACT.Sigmoid, scale=steep_sb[:, r : r + 1])
+                nc.scalar.activation(gate[:, rr, :], contrast[b][:, rr, :], ACT.Sigmoid, scale=steep_per_member[:, r : r + 1])
             for rr in range(2):
                 r = 2 * b + rr
                 nc.scalar.activation(weight_rows[:, r, :], gate[:, rr, :], ACT.Copy, scale=us_sb[:, r : r + 1])
         weight_grouped = sb.tile([P, Q, PACK], BF16, name="weight_grouped", align_bytes=64)
         nc.scalar.copy(
             weight_grouped[:].rearrange("p (c i) r -> p c r i", i=4),
-            weight_rows[:].rearrange("p r (c i) -> p c r i", i=4),
+            weight_rows.rearrange("p r (c i) -> p c r i", i=4),
         )
-        weight_codes = sb.tile([P, Q], U32, name="weight_codes", align_bytes=64)
+        late_codes = sb.tile([P, Q + 3 * P], U32, name="late_codes", tag="plane3", align_bytes=64)
+        weight_codes = late_codes[:, :Q]
         weight_scales = sb.tile([P, Q], U8, name="weight_scales", align_bytes=64)
         nc.vector.quantize_mx(
-            out=weight_codes[:].bitcast(FP8X4), scales=weight_scales[:], in_=weight_grouped[:].rearrange("p q r -> p (q r)")
+            out=weight_codes.bitcast(FP8X4), scales=weight_scales[:], in_=weight_grouped[:].rearrange("p q r -> p (q r)")
         )
 
-        result = [ps.tile([P, PACK, HALF], F32, name="result%d" % h) for h in range(2)]
         out_rows = out_0.rearrange("(p t) q -> p t q", t=PACK)
-        result_sb = [sb.tile([P, Q], F32, name="result_sb%d" % t) for t in range(PACK)]
-        for t in range(PACK):
-            val_listed = sb.tile([P, I], BF16, name="val_listed%d" % t)
-            nc.vector.tensor_copy(val_listed[:], val_pool[t][:].indirect(offsets[:]))
-            pairs = val_listed[:].bitcast(F32)
+
+        first_listed = sb.tile([P, I], BF16, name="first_listed")
+        first_grouped = sb.tile([P, I], BF16, name="first_grouped", align_bytes=64)
+        first_codes = sb.tile([P, P], U32, name="first_codes", align_bytes=64)
+
+        def quantize_values(t):
+            val_listed = late_listed[:, (t - 1) * I : t * I] if t else first_listed[:]
+            val_grouped = late_grouped[:, (t - 1) * I : t * I] if t else first_grouped[:]
+            val_codes = late_codes[:, Q + (t - 1) * P : Q + t * P] if t else first_codes[:]
+            nc.vector.tensor_copy(val_listed, val_pool[t][:].indirect(offsets[:]))
+            pairs = val_listed.bitcast(F32)
             turned = ps.tile([P, 2, P], F32, name="turned%d" % t)
             for u in range(2):
                 nc.tensor.transpose(turned[:, u, :], pairs[:, u : I // 2 : 2], identity[:])
-            val_grouped = sb.tile([P, P, PACK], BF16, name="val_grouped%d" % t, align_bytes=64)
-            nc.scalar.copy(val_grouped[:].bitcast(F32), turned[:].rearrange("p u c -> p c u"))
-            val_codes = sb.tile([P, P], U32, name="val_codes%d" % t, align_bytes=64)
+            nc.scalar.copy(val_grouped.bitcast(F32).rearrange("p (c u) -> p c u", u=2), turned[:].rearrange("p u c -> p c u"))
             val_scales = sb.tile([P, P], U8, name="val_scales%d" % t, align_bytes=64)
-            nc.vector.quantize_mx(
-                out=val_codes[:].bitcast(FP8X4), scales=val_scales[:], in_=val_grouped[:].rearrange("p c r -> p (c r)")
+            nc.vector.quantize_mx(out=val_codes.bitcast(FP8X4), scales=val_scales[:], in_=val_grouped)
+            return val_codes, val_scales
+
+        result_sb = sb.tile([P, PACK * Q], F32, name="result_sb")
+        banks = [ps.tile([P, Q], F32, name="result%d" % t, tag="scores%d" % t if t < 2 else "result%d" % t) for t in range(PACK)]
+        for t in range(PACK):
+            val_codes, val_scales = quantize_values(t)
+            nc.tensor.matmul_mx(
+                out=banks[t][:],
+                lhsT=val_codes.bitcast(FP8X4),
+                lhsT_scale=val_scales[:],
+                rhs=weight_codes.bitcast(FP8X4),
+                rhs_scale=weight_scales[:],
+                start=True,
+                stop=True,
             )
-            for h in range(2):
-                cols = slice(h * HALF, (h + 1) * HALF)
-                nc.tensor.matmul_mx(
-                    out=result[h][:, t, :],
-                    lhsT=val_codes[:].bitcast(FP8X4),
-                    lhsT_scale=val_scales[:],
-                    rhs=weight_codes[:, cols].bitcast(FP8X4),
-                    rhs_scale=weight_scales[:, cols],
-                    start=True,
-                    stop=True,
-                )
-            if t < PACK - 1:
-                for h in range(2):
-                    nc.scalar.copy(result_sb[t][:, h * HALF : (h + 1) * HALF], result[h][:, t, :])
-                nc.sync.dma_start(out_rows[:, t, :], result_sb[t][:])
+            nc.scalar.copy(result_sb[:, t * Q : (t + 1) * Q], banks[t][:])
+        result_rows = result_sb[:].rearrange("p (t q) -> p t q", t=PACK)
+        nc.sync.dma_start(out_rows[:, :last, :], result_rows[:, :last, :])
+        nc.sync.dma_start(out_rows[:, last, :], result_rows[:, last, :])
 
-        result_grouped = [sb.tile([P, HALF, PACK], BF16, name="result_grouped%d" % h, align_bytes=64) for h in range(2)]
-        nc.vector.tensor_copy(result_grouped[0][:], result[0][:].rearrange("p t q -> p q t"))
-        nc.scalar.copy(result_grouped[1][:], result[1][:].rearrange("p t q -> p q t"))
-        last = PACK - 1
-        for h in (1, 0):
-            nc.scalar.copy(result_sb[last][:, h * HALF : (h + 1) * HALF], result[h][:, last, :])
-        nc.scalar.dma_start(out_rows[:, last, :], result_sb[last][:])
-
+        result_grouped = sb.tile([P, Q, PACK], BF16, name="result_grouped", align_bytes=64)
+        for cols, copy in ((slice(0, 160), nc.vector.tensor_copy), (slice(160, Q), nc.scalar.copy)):
+            copy(
+                result_grouped[:, cols, :].rearrange("p (c i) t -> p c t i", i=4),
+                result_rows[:, :, cols].rearrange("p t (c i) -> p c t i", i=4),
+            )
         result_codes = sb.tile([P, Q], U32, name="result_codes", align_bytes=64)
         result_scales = sb.tile([P, Q], U8, name="result_scales", align_bytes=64)
-        for h in range(2):
-            cols = slice(h * HALF, (h + 1) * HALF)
-            nc.vector.quantize_mx(
-                out=result_codes[:, cols].bitcast(FP8X4),
-                scales=result_scales[:, cols],
-                in_=result_grouped[h][:].rearrange("p q t -> p (q t)"),
-            )
+        nc.vector.quantize_mx(
+            out=result_codes[:].bitcast(FP8X4), scales=result_scales[:], in_=result_grouped[:].rearrange("p q t -> p (q t)")
+        )
         nc.sync.dma_start(out_1[0].rearrange("p q t -> p (q t)").bitcast(I32), result_codes[:].bitcast(I32))
         for quad in range(4):
             queue = nc.sync if quad < 2 else nc.scalar

@@ -19,7 +19,16 @@ ALU = mybir.AluOpType
 
 P = 128
 PACK = 4
-HALF = Q // 2
+QUADRANTS = 4
+SCALE_ROWS = 4
+TILES_PER_BANK = 2
+LAST = PACK - 1
+MX_ALIGN = 64
+VECTOR_COLUMNS = 160
+
+
+def interleave(copy, out, in_):
+    copy(out.rearrange("p (c i) j -> p c j i", i=4), in_.rearrange("p j (c i) -> p c j i", i=4))
 
 
 def tile_attend_teamcontrast_pl_kernel(tc, query, keys_words, keys_scales, steep, us, vals, offs, out_0, out_1, out_2):
@@ -28,72 +37,67 @@ def tile_attend_teamcontrast_pl_kernel(tc, query, keys_words, keys_scales, steep
         sb = ctx.enter_context(tc.tile_pool(name="sb", bufs=1))
         ps = ctx.enter_context(tc.psum_pool(name="ps", bufs=1))
 
+        def on_plane(t, shape, dtype, name):
+            return sb.tile(shape, dtype, name=name, tag="plane%d" % t, align_bytes=MX_ALIGN)
+
         offsets = sb.tile([P, I // 16], U16, name="offsets")
-        key_pool = sb.tile([P, T], U16, name="key_pool", tag="plane1")
-        key_scale_pool = sb.tile([P, T], U8, name="key_scale_pool", tag="plane2")
-        query_raw = sb.tile([P, PACK, Q], F32, name="query_raw", tag="plane3", align_bytes=64)
-        steep_sb = sb.tile([P, PACK], F32, name="steep_sb", tag="plane0")
+        key_pool = on_plane(1, [P, T], U16, "key_pool")
+        key_scale_pool = on_plane(2, [P, T], U8, "key_scale_pool")
+        warmup_in = on_plane(LAST, [P, 1], F32, "warmup_in")
+        query_raw = on_plane(LAST, [P, PACK, Q], F32, "query_raw")
+        steep_sb = on_plane(0, [P, PACK], F32, "steep_sb")
         us_sb = sb.tile([P, PACK], F32, name="us_sb")
         identity = sb.tile([P, P], F32, name="identity")
-        warmup_in = sb.tile([P, 1], F32, name="warmup_in")
         warmup_out = sb.tile([P, 1], F32, name="warmup_out")
+
         nc.vector.memset(key_scale_pool[:].bitcast(I32), 0)
-        nc.vector.memset(warmup_in[:], 0.0)
+        nc.gpsimd.memset(warmup_in[:], 0.0)
         nc.scalar.activation(warmup_out[:], warmup_in[:], ACT.Sigmoid)
         make_identity(nc, identity[:])
+
         nc.sync.dma_start(offsets[:], offs)
-        nc.sync.dma_start(steep_sb[:], steep.rearrange("(p r) o -> p (r o)", r=PACK))
-        nc.gpsimd.dma_start(us_sb[:], us.rearrange("(p r) o -> p (r o)", r=PACK))
+        nc.sync.dma_start(steep_sb[:], steep.rearrange("(s r) o -> s (r o)", r=PACK))
+        nc.gpsimd.dma_start(us_sb[:], us.rearrange("(s r) o -> s (r o)", r=PACK))
         nc.sync.dma_start(key_pool[:].bitcast(I32), keys_words[0].bitcast(I32))
-        nc.sync.dma_start(query_raw[:], query.rearrange("(p j) q -> p j q", j=PACK))
-        for quad in range(4):
+        for quad in range(QUADRANTS):
             nc.sync.dma_start(
-                key_scale_pool[32 * quad : 32 * quad + 4, :].bitcast(I32),
-                keys_scales[0, 4 * quad : 4 * quad + 4, :].bitcast(I32),
+                key_scale_pool[32 * quad : 32 * quad + SCALE_ROWS, :].bitcast(I32),
+                keys_scales[0, SCALE_ROWS * quad : SCALE_ROWS * (quad + 1), :].bitcast(I32),
             )
+        nc.sync.dma_start(query_raw[:], query.rearrange("(p j) q -> p j q", j=PACK))
         steep_per_member = sb.tile([P, PACK], F32, name="steep_per_member")
         nc.vector.tensor_scalar(out=steep_per_member[:], in0=steep_sb[:], scalar1=1.0 / TEAM, scalar2=None, op0=ALU.mult)
         vals_planes = vals.rearrange("(p t) n -> t p n", t=PACK)
-
-        def load_values(t):
-            if t == PACK - 1:
-                plane = sb.tile([P, T], F32, name="val_pool%d" % t, tag="plane%d" % t, align_bytes=64)
-            else:
-                plane = sb.tile([P, T], F32, name="val_pool%d" % t, tag="plane%d" % t)
-            nc.sync.dma_start(plane[:], vals_planes[t])
-            return plane
-
-        val_pool = [load_values(t) for t in range(PACK)]
+        val_pool = [on_plane(t, [P, T], F32, "val_pool%d" % t) for t in range(PACK)]
+        for t in range(PACK):
+            nc.sync.dma_start(val_pool[t][:], vals_planes[t])
 
         key_listed = sb.tile([P, I], U16, name="key_listed")
         key_scale_listed = sb.tile([P, I], U8, name="key_scale_listed")
         nc.vector.tensor_copy(key_listed[:], key_pool[:].indirect(offsets[:]))
         nc.vector.tensor_copy(key_scale_listed[:], key_scale_pool[:].indirect(offsets[:]))
-        key_dealt = sb.tile([P, PACK, P], U16, name="key_dealt", align_bytes=64)
-        key_scale_dealt = sb.tile([P, PACK, P], U8, name="key_scale_dealt", align_bytes=64)
+        key_dealt = sb.tile([P, PACK, P], U16, name="key_dealt", align_bytes=MX_ALIGN)
+        key_scale_dealt = sb.tile([P, PACK, P], U8, name="key_scale_dealt", align_bytes=MX_ALIGN)
         nc.vector.tensor_copy(key_dealt[:], key_listed[:].rearrange("p (s r) -> p r s", r=PACK))
         nc.vector.tensor_copy(key_scale_dealt[:], key_scale_listed[:].rearrange("p (s r) -> p r s", r=PACK))
 
-        query_grouped = sb.tile([P, Q, PACK], BF16, name="query_grouped", align_bytes=64)
-        nc.scalar.copy(
-            query_grouped[:].rearrange("p (c i) j -> p c j i", i=4),
-            query_raw[:].rearrange("p j (c i) -> p c j i", i=4),
-        )
-        query_codes = sb.tile([P, Q], U32, name="query_codes", align_bytes=64)
-        query_scales = sb.tile([P, Q], U8, name="query_scales", align_bytes=64)
+        query_grouped = sb.tile([P, Q, PACK], BF16, name="query_grouped", align_bytes=MX_ALIGN)
+        interleave(nc.scalar.copy, query_grouped[:], query_raw[:])
+        query_codes = sb.tile([P, Q], U32, name="query_codes", align_bytes=MX_ALIGN)
+        query_scales = sb.tile([P, Q], U8, name="query_scales", align_bytes=MX_ALIGN)
         nc.vector.quantize_mx(
             out=query_codes[:].bitcast(FP8X4), scales=query_scales[:], in_=query_grouped[:].rearrange("p q j -> p (q j)")
         )
 
-        last = PACK - 1
-        late_listed = sb.tile([P, last * I], BF16, name="late_listed", tag="plane0")
-        late_grouped = sb.tile([P, last * I], BF16, name="late_grouped", align_bytes=64)
-        weight_rows = late_grouped[:, Q : Q + PACK * Q].rearrange("p (r q) -> p r q", r=PACK)
-        teams = 2 * Q // TEAM
-        scores = [ps.tile([P, 2, Q], F32, name="scores%d" % b, tag="scores%d" % b) for b in range(2)]
+        late_listed = on_plane(0, [P, LAST * I], BF16, "late_listed")
+        late_grouped = sb.tile([P, LAST * I], BF16, name="late_grouped", align_bytes=MX_ALIGN)
+        weight_rows = late_grouped[:, I // 2 : I // 2 + PACK * Q].rearrange("p (r q) -> p r q", r=PACK)
+        banks = range(PACK // TILES_PER_BANK)
+        teams = TILES_PER_BANK * Q // TEAM
+        scores = [ps.tile([P, TILES_PER_BANK, Q], F32, name="scores%d" % b, tag="scores%d" % b) for b in banks]
         for r in range(PACK):
             nc.tensor.matmul_mx(
-                out=scores[r // 2][:, r % 2, :],
+                out=scores[r // TILES_PER_BANK][:, r % TILES_PER_BANK, :],
                 lhsT=key_dealt[:, r, :].bitcast(FP4X4),
                 lhsT_scale=key_scale_dealt[:, r, :],
                 rhs=query_codes[:].bitcast(FP8X4),
@@ -101,12 +105,12 @@ def tile_attend_teamcontrast_pl_kernel(tc, query, keys_words, keys_scales, steep
                 start=True,
                 stop=True,
             )
-        by_team = [scores[b][:].rearrange("p r (g m) -> p (r g) m", m=TEAM) for b in range(2)]
+        by_team = [scores[b][:].rearrange("p r (g m) -> p (r g) m", m=TEAM) for b in banks]
         team_sum = [late_listed[:, : 2 * teams].bitcast(F32), late_listed[:, I - teams : I + teams].bitcast(F32)]
-        contrast = [sb.tile([P, 2, Q], F32, name="contrast%d" % b) for b in range(2)]
-        for b in range(2):
+        contrast = [sb.tile([P, TILES_PER_BANK, Q], F32, name="contrast%d" % b) for b in banks]
+        for b in banks:
             nc.vector.tensor_reduce(out=team_sum[b], in_=by_team[b], axis=mybir.AxisListType.X, op=ALU.add)
-        for b in range(2):
+        for b in banks:
             nc.vector.scalar_tensor_tensor(
                 out=contrast[b][:].rearrange("p r (g m) -> p (r g) m", m=TEAM),
                 in0=by_team[b],
@@ -115,31 +119,26 @@ def tile_attend_teamcontrast_pl_kernel(tc, query, keys_words, keys_scales, steep
                 op0=ALU.mult,
                 op1=ALU.subtract,
             )
-        for b in range(2):
-            gate = sb.tile([P, 2, Q], F32, name="gate%d" % b)
-            for rr in range(2):
-                r = 2 * b + rr
-                nc.scalar.activation(gate[:, rr, :], contrast[b][:, rr, :], ACT.Sigmoid, scale=steep_per_member[:, r : r + 1])
-            for rr in range(2):
-                r = 2 * b + rr
-                nc.scalar.activation(weight_rows[:, r, :], gate[:, rr, :], ACT.Copy, scale=us_sb[:, r : r + 1])
-        weight_grouped = sb.tile([P, Q, PACK], BF16, name="weight_grouped", align_bytes=64)
-        nc.scalar.copy(
-            weight_grouped[:].rearrange("p (c i) r -> p c r i", i=4),
-            weight_rows.rearrange("p r (c i) -> p c r i", i=4),
-        )
-        late_codes = sb.tile([P, Q + 3 * P], U32, name="late_codes", tag="plane3", align_bytes=64)
+        for b in banks:
+            gate = sb.tile([P, TILES_PER_BANK, Q], F32, name="gate%d" % b)
+            for k in range(TILES_PER_BANK):
+                r = TILES_PER_BANK * b + k
+                nc.scalar.activation(gate[:, k, :], contrast[b][:, k, :], ACT.Sigmoid, scale=steep_per_member[:, r : r + 1])
+            for k in range(TILES_PER_BANK):
+                r = TILES_PER_BANK * b + k
+                nc.scalar.activation(weight_rows[:, r, :], gate[:, k, :], ACT.Copy, scale=us_sb[:, r : r + 1])
+        weight_grouped = sb.tile([P, Q, PACK], BF16, name="weight_grouped", align_bytes=MX_ALIGN)
+        interleave(nc.scalar.copy, weight_grouped[:], weight_rows)
+        late_codes = on_plane(LAST, [P, Q + LAST * P], U32, "late_codes")
         weight_codes = late_codes[:, :Q]
-        weight_scales = sb.tile([P, Q], U8, name="weight_scales", align_bytes=64)
+        weight_scales = sb.tile([P, Q], U8, name="weight_scales", align_bytes=MX_ALIGN)
         nc.vector.quantize_mx(
             out=weight_codes.bitcast(FP8X4), scales=weight_scales[:], in_=weight_grouped[:].rearrange("p q r -> p (q r)")
         )
 
-        out_rows = out_0.rearrange("(p t) q -> p t q", t=PACK)
-
         first_listed = sb.tile([P, I], BF16, name="first_listed")
-        first_grouped = sb.tile([P, I], BF16, name="first_grouped", align_bytes=64)
-        first_codes = sb.tile([P, P], U32, name="first_codes", align_bytes=64)
+        first_grouped = sb.tile([P, I], BF16, name="first_grouped", align_bytes=MX_ALIGN)
+        first_codes = sb.tile([P, P], U32, name="first_codes", align_bytes=MX_ALIGN)
 
         def quantize_values(t):
             val_listed = late_listed[:, (t - 1) * I : t * I] if t else first_listed[:]
@@ -150,17 +149,19 @@ def tile_attend_teamcontrast_pl_kernel(tc, query, keys_words, keys_scales, steep
             turned = ps.tile([P, 2, P], F32, name="turned%d" % t)
             for u in range(2):
                 nc.tensor.transpose(turned[:, u, :], pairs[:, u : I // 2 : 2], identity[:])
-            nc.scalar.copy(val_grouped.bitcast(F32).rearrange("p (c u) -> p c u", u=2), turned[:].rearrange("p u c -> p c u"))
-            val_scales = sb.tile([P, P], U8, name="val_scales%d" % t, align_bytes=64)
+            nc.scalar.copy(val_grouped.bitcast(F32).rearrange("s (p u) -> s p u", u=2), turned[:].rearrange("s u p -> s p u"))
+            val_scales = sb.tile([P, P], U8, name="val_scales%d" % t, align_bytes=MX_ALIGN)
             nc.vector.quantize_mx(out=val_codes.bitcast(FP8X4), scales=val_scales[:], in_=val_grouped)
             return val_codes, val_scales
 
         result_sb = sb.tile([P, PACK * Q], F32, name="result_sb")
-        banks = [ps.tile([P, Q], F32, name="result%d" % t, tag="scores%d" % t if t < 2 else "result%d" % t) for t in range(PACK)]
+        result = [
+            ps.tile([P, Q], F32, name="result%d" % t, tag="scores%d" % t if t in banks else "result%d" % t) for t in range(PACK)
+        ]
         for t in range(PACK):
             val_codes, val_scales = quantize_values(t)
             nc.tensor.matmul_mx(
-                out=banks[t][:],
+                out=result[t][:],
                 lhsT=val_codes.bitcast(FP8X4),
                 lhsT_scale=val_scales[:],
                 rhs=weight_codes.bitcast(FP8X4),
@@ -168,26 +169,24 @@ def tile_attend_teamcontrast_pl_kernel(tc, query, keys_words, keys_scales, steep
                 start=True,
                 stop=True,
             )
-            nc.scalar.copy(result_sb[:, t * Q : (t + 1) * Q], banks[t][:])
+            nc.scalar.copy(result_sb[:, t * Q : (t + 1) * Q], result[t][:])
         result_rows = result_sb[:].rearrange("p (t q) -> p t q", t=PACK)
-        nc.sync.dma_start(out_rows[:, :last, :], result_rows[:, :last, :])
-        nc.sync.dma_start(out_rows[:, last, :], result_rows[:, last, :])
+        out_rows = out_0.rearrange("(p t) q -> p t q", t=PACK)
+        nc.sync.dma_start(out_rows[:, :LAST, :], result_rows[:, :LAST, :])
+        nc.sync.dma_start(out_rows[:, LAST, :], result_rows[:, LAST, :])
 
-        result_grouped = sb.tile([P, Q, PACK], BF16, name="result_grouped", align_bytes=64)
-        for cols, copy in ((slice(0, 160), nc.vector.tensor_copy), (slice(160, Q), nc.scalar.copy)):
-            copy(
-                result_grouped[:, cols, :].rearrange("p (c i) t -> p c t i", i=4),
-                result_rows[:, :, cols].rearrange("p t (c i) -> p c t i", i=4),
-            )
-        result_codes = sb.tile([P, Q], U32, name="result_codes", align_bytes=64)
-        result_scales = sb.tile([P, Q], U8, name="result_scales", align_bytes=64)
+        result_grouped = sb.tile([P, Q, PACK], BF16, name="result_grouped", align_bytes=MX_ALIGN)
+        for cols, copy in ((slice(0, VECTOR_COLUMNS), nc.vector.tensor_copy), (slice(VECTOR_COLUMNS, Q), nc.scalar.copy)):
+            interleave(copy, result_grouped[:, cols, :], result_rows[:, :, cols])
+        result_codes = sb.tile([P, Q], U32, name="result_codes", align_bytes=MX_ALIGN)
+        result_scales = sb.tile([P, Q], U8, name="result_scales", align_bytes=MX_ALIGN)
         nc.vector.quantize_mx(
             out=result_codes[:].bitcast(FP8X4), scales=result_scales[:], in_=result_grouped[:].rearrange("p q t -> p (q t)")
         )
         nc.sync.dma_start(out_1[0].rearrange("p q t -> p (q t)").bitcast(I32), result_codes[:].bitcast(I32))
-        for quad in range(4):
-            queue = nc.sync if quad < 2 else nc.scalar
+        for quad in range(QUADRANTS):
+            queue = nc.sync if quad < QUADRANTS // 2 else nc.scalar
             queue.dma_start(
-                out_2[0, 4 * quad : 4 * quad + 4, :].bitcast(I32),
-                result_scales[32 * quad : 32 * quad + 4, :].bitcast(I32),
+                out_2[0, SCALE_ROWS * quad : SCALE_ROWS * (quad + 1), :].bitcast(I32),
+                result_scales[32 * quad : 32 * quad + SCALE_ROWS, :].bitcast(I32),
             )

@@ -24,7 +24,6 @@ SCALE_ROWS = 4
 TILES_PER_BANK = 2
 LAST = PACK - 1
 MX_ALIGN = 64
-VECTOR_COLUMNS = 160
 
 
 def interleave(copy, out, in_):
@@ -154,30 +153,41 @@ def tile_attend_teamcontrast_pl_kernel(tc, query, keys_words, keys_scales, steep
             nc.vector.quantize_mx(out=val_codes.bitcast(FP8X4), scales=val_scales[:], in_=val_grouped)
             return val_codes, val_scales
 
-        result_sb = sb.tile([P, PACK * Q], F32, name="result_sb")
-        result = [
-            ps.tile([P, Q], F32, name="result%d" % t, tag="scores%d" % t if t in banks else "result%d" % t) for t in range(PACK)
-        ]
-        for t in range(PACK):
-            val_codes, val_scales = quantize_values(t)
+        def multiply(out, val_codes, val_scales, cols):
             nc.tensor.matmul_mx(
-                out=result[t][:],
+                out=out,
                 lhsT=val_codes.bitcast(FP8X4),
                 lhsT_scale=val_scales[:],
-                rhs=weight_codes.bitcast(FP8X4),
-                rhs_scale=weight_scales[:],
+                rhs=weight_codes[:, cols].bitcast(FP8X4),
+                rhs_scale=weight_scales[:, cols],
                 start=True,
                 stop=True,
             )
-            nc.scalar.copy(result_sb[:, t * Q : (t + 1) * Q], result[t][:])
-        result_rows = result_sb[:].rearrange("p (t q) -> p t q", t=PACK)
-        out_rows = out_0.rearrange("(p t) q -> p t q", t=PACK)
-        nc.sync.dma_start(out_rows[:, :LAST, :], result_rows[:, :LAST, :])
-        nc.sync.dma_start(out_rows[:, LAST, :], result_rows[:, LAST, :])
 
+        result_sb = sb.tile([P, PACK * Q], F32, name="result_sb")
+        result_rows = result_sb[:].rearrange("p (t q) -> p t q", t=PACK)
         result_grouped = sb.tile([P, Q, PACK], BF16, name="result_grouped", align_bytes=MX_ALIGN)
-        for cols, copy in ((slice(0, VECTOR_COLUMNS), nc.vector.tensor_copy), (slice(VECTOR_COLUMNS, Q), nc.scalar.copy)):
-            interleave(copy, result_grouped[:, cols, :], result_rows[:, :, cols])
+        out_rows = out_0.rearrange("(p t) q -> p t q", t=PACK)
+
+        early = ps.tile([P, 2, Q], F32, name="early", tag="scores0")
+        for t in range(2):
+            multiply(early[:, t, :], *quantize_values(t), slice(0, Q))
+        nc.scalar.copy(result_rows[:, :2, :], early[:])
+        nc.sync.dma_start(out_rows[:, :2, :], result_rows[:, :2, :])
+        nc.vector.tensor_copy(result_grouped[:, :, :2], result_rows[:, :2, :].rearrange("p t q -> p q t"))
+
+        halves = [slice(0, Q // 2), slice(Q // 2, Q)]
+        late = [ps.tile([P, 2, Q // 2], F32, name="late%d" % h, tag=("scores1", "late1")[h]) for h in range(2)]
+        for t in range(2, PACK):
+            val_codes, val_scales = quantize_values(t)
+            for h in range(2):
+                multiply(late[h][:, t - 2, :], val_codes, val_scales, halves[h])
+        for h, copy in enumerate((nc.vector.tensor_copy, nc.scalar.copy)):
+            copy(result_grouped[:, halves[h], 2:], late[h][:].rearrange("p t q -> p q t"))
+        for h in (1, 0):
+            nc.scalar.copy(result_rows[:, 2:, halves[h]], late[h][:])
+        nc.scalar.dma_start(out_rows[:, 2:, :], result_rows[:, 2:, :])
+
         result_codes = sb.tile([P, Q], U32, name="result_codes", align_bytes=MX_ALIGN)
         result_scales = sb.tile([P, Q], U8, name="result_scales", align_bytes=MX_ALIGN)
         nc.vector.quantize_mx(

from contextlib import ExitStack

import concourse.mybir as mybir
from concourse.masks import make_identity

D, T, I, Q, TEAM, E = 512, 2048, 512, 256, 8, 512
FLOPS = 2 * D * I * Q + 2 * I * E * Q

F32 = mybir.dt.float32
BF16 = mybir.dt.bfloat16
I32 = mybir.dt.int32
U32 = mybir.dt.uint32
U16 = mybir.dt.uint16
U8 = mybir.dt.uint8
FP8X4 = mybir.dt.float8_e4m3fn_x4
FP4X4 = mybir.dt.float4_e2m1fn_x4
ACT = mybir.ActivationFunctionType
ALU = mybir.AluOpType

P = 128
PACK = 4
QUADRANTS = 4
SCALE_ROWS = 4
TILES_PER_BANK = 2
LAST = PACK - 1
MX_ALIGN = 64


def interleave(copy, out, in_):
    copy(out.rearrange("p (c i) j -> p c j i", i=4), in_.rearrange("p j (c i) -> p c j i", i=4))


def tile_attend_teamcontrast_pl_kernel(tc, query, keys_words, keys_scales, steep, us, vals, offs, out_0, out_1, out_2):
    nc = tc.nc
    with ExitStack() as ctx:
        sb = ctx.enter_context(tc.tile_pool(name="sb", bufs=1))
        ps = ctx.enter_context(tc.psum_pool(name="ps", bufs=1))

        def on_plane(t, shape, dtype, name):
            return sb.tile(shape, dtype, name=name, tag="plane%d" % t, align_bytes=MX_ALIGN)

        offsets = sb.tile([P, I // 16], U16, name="offsets")
        key_pool = on_plane(1, [P, T], U16, "key_pool")
        key_scale_pool = on_plane(2, [P, T], U8, "key_scale_pool")
        warmup_in = on_plane(LAST, [P, 1], F32, "warmup_in")
        query_raw = on_plane(LAST, [P, PACK, Q], F32, "query_raw")
        steep_sb = on_plane(0, [P, PACK], F32, "steep_sb")
        us_sb = sb.tile([P, PACK], F32, name="us_sb")
        identity = sb.tile([P, P], F32, name="identity")
        warmup_out = sb.tile([P, 1], F32, name="warmup_out")

        nc.vector.memset(key_scale_pool[:].bitcast(I32), 0)
        nc.gpsimd.memset(warmup_in[:], 0.0)
        nc.scalar.activation(warmup_out[:], warmup_in[:], ACT.Sigmoid)
        make_identity(nc, identity[:])

        nc.sync.dma_start(offsets[:], offs)
        nc.sync.dma_start(steep_sb[:], steep.rearrange("(s r) o -> s (r o)", r=PACK))
        nc.gpsimd.dma_start(us_sb[:], us.rearrange("(s r) o -> s (r o)", r=PACK))
        nc.sync.dma_start(key_pool[:].bitcast(I32), keys_words[0].bitcast(I32))
        for quad in range(QUADRANTS):
            nc.sync.dma_start(
                key_scale_pool[32 * quad : 32 * quad + SCALE_ROWS, :].bitcast(I32),
                keys_scales[0, SCALE_ROWS * quad : SCALE_ROWS * (quad + 1), :].bitcast(I32),
            )
        nc.sync.dma_start(query_raw[:], query.rearrange("(p j) q -> p j q", j=PACK))
        steep_per_member = sb.tile([P, PACK], F32, name="steep_per_member")
        nc.vector.tensor_scalar(out=steep_per_member[:], in0=steep_sb[:], scalar1=1.0 / TEAM, scalar2=None, op0=ALU.mult)
        vals_planes = vals.rearrange("(p t) n -> t p n", t=PACK)
        val_pool = [on_plane(t, [P, T], F32, "val_pool%d" % t) for t in range(PACK)]
        for t in range(PACK):
            nc.sync.dma_start(val_pool[t][:], vals_planes[t])

        key_listed = sb.tile([P, I], U16, name="key_listed")
        key_scale_listed = sb.tile([P, I], U8, name="key_scale_listed")
        nc.vector.tensor_copy(key_listed[:], key_pool[:].indirect(offsets[:]))
        nc.vector.tensor_copy(key_scale_listed[:], key_scale_pool[:].indirect(offsets[:]))
        key_dealt = sb.tile([P, PACK, P], U16, name="key_dealt", align_bytes=MX_ALIGN)
        key_scale_dealt = sb.tile([P, PACK, P], U8, name="key_scale_dealt", align_bytes=MX_ALIGN)
        nc.vector.tensor_copy(key_dealt[:], key_listed[:].rearrange("p (s r) -> p r s", r=PACK))
        nc.vector.tensor_copy(key_scale_dealt[:], key_scale_listed[:].rearrange("p (s r) -> p r s", r=PACK))

        query_grouped = sb.tile([P, Q, PACK], BF16, name="query_grouped", align_bytes=MX_ALIGN)
        interleave(nc.scalar.copy, query_grouped[:], query_raw[:])
        query_codes = sb.tile([P, Q], U32, name="query_codes", align_bytes=MX_ALIGN)
        query_scales = sb.tile([P, Q], U8, name="query_scales", align_bytes=MX_ALIGN)
        nc.vector.quantize_mx(
            out=query_codes[:].bitcast(FP8X4), scales=query_scales[:], in_=query_grouped[:].rearrange("p q j -> p (q j)")
        )

        late_listed = on_plane(0, [P, LAST * I], BF16, "late_listed")
        late_grouped = sb.tile([P, LAST * I], BF16, name="late_grouped", align_bytes=MX_ALIGN)
        weight_rows = late_grouped[:, I // 2 : I // 2 + PACK * Q].rearrange("p (r q) -> p r q", r=PACK)
        banks = range(PACK // TILES_PER_BANK)
        teams = TILES_PER_BANK * Q // TEAM
        scores = [ps.tile([P, TILES_PER_BANK, Q], F32, name="scores%d" % b, tag="scores%d" % b) for b in banks]
        for r in range(PACK):
            nc.tensor.matmul_mx(
                out=scores[r // TILES_PER_BANK][:, r % TILES_PER_BANK, :],
                lhsT=key_dealt[:, r, :].bitcast(FP4X4),
                lhsT_scale=key_scale_dealt[:, r, :],
                rhs=query_codes[:].bitcast(FP8X4),
                rhs_scale=query_scales[:],
                start=True,
                stop=True,
            )
        by_team = [scores[b][:].rearrange("p r (g m) -> p (r g) m", m=TEAM) for b in banks]
        team_sum = [late_listed[:, : 2 * teams].bitcast(F32), late_listed[:, I - teams : I + teams].bitcast(F32)]
        contrast = [sb.tile([P, TILES_PER_BANK, Q], F32, name="contrast%d" % b) for b in banks]
        for b in banks:
            nc.vector.tensor_reduce(out=team_sum[b], in_=by_team[b], axis=mybir.AxisListType.X, op=ALU.add)
        for b in banks:
            nc.vector.scalar_tensor_tensor(
                out=contrast[b][:].rearrange("p r (g m) -> p (r g) m", m=TEAM),
                in0=by_team[b],
                scalar=float(TEAM),
                in1=team_sum[b].unsqueeze(2).to_broadcast([P, teams, TEAM]),
                op0=ALU.mult,
                op1=ALU.subtract,
            )
        for b in banks:
            gate = sb.tile([P, TILES_PER_BANK, Q], F32, name="gate%d" % b)
            for k in range(TILES_PER_BANK):
                r = TILES_PER_BANK * b + k
                nc.scalar.activation(gate[:, k, :], contrast[b][:, k, :], ACT.Sigmoid, scale=steep_per_member[:, r : r + 1])
            for k in range(TILES_PER_BANK):
                r = TILES_PER_BANK * b + k
                nc.scalar.activation(weight_rows[:, r, :], gate[:, k, :], ACT.Copy, scale=us_sb[:, r : r + 1])
        weight_grouped = sb.tile([P, Q, PACK], BF16, name="weight_grouped", align_bytes=MX_ALIGN)
        interleave(nc.scalar.copy, weight_grouped[:], weight_rows)
        late_codes = on_plane(LAST, [P, Q + LAST * P], U32, "late_codes")
        weight_codes = late_codes[:, :Q]
        weight_scales = sb.tile([P, Q], U8, name="weight_scales", align_bytes=MX_ALIGN)
        nc.vector.quantize_mx(
            out=weight_codes.bitcast(FP8X4), scales=weight_scales[:], in_=weight_grouped[:].rearrange("p q r -> p (q r)")
        )

        first_listed = sb.tile([P, I], BF16, name="first_listed")
        first_grouped = sb.tile([P, I], BF16, name="first_grouped", align_bytes=MX_ALIGN)
        first_codes = sb.tile([P, P], U32, name="first_codes", align_bytes=MX_ALIGN)

        def quantize_values(t):
            val_listed = late_listed[:, (t - 1) * I : t * I] if t else first_listed[:]
            val_grouped = late_grouped[:, (t - 1) * I : t * I] if t else first_grouped[:]
            val_codes = late_codes[:, Q + (t - 1) * P : Q + t * P] if t else first_codes[:]
            nc.vector.tensor_copy(val_listed, val_pool[t][:].indirect(offsets[:]))
            pairs = val_listed.bitcast(F32)
            turned = ps.tile([P, 2, P], F32, name="turned%d" % t)
            for u in range(2):
                nc.tensor.transpose(turned[:, u, :], pairs[:, u : I // 2 : 2], identity[:])
            nc.scalar.copy(val_grouped.bitcast(F32).rearrange("s (p u) -> s p u", u=2), turned[:].rearrange("s u p -> s p u"))
            val_scales = sb.tile([P, P], U8, name="val_scales%d" % t, align_bytes=MX_ALIGN)
            nc.vector.quantize_mx(out=val_codes.bitcast(FP8X4), scales=val_scales[:], in_=val_grouped)
            return val_codes, val_scales

        def multiply(out, val_codes, val_scales, cols):
            nc.tensor.matmul_mx(
                out=out,
                lhsT=val_codes.bitcast(FP8X4),
                lhsT_scale=val_scales[:],
                rhs=weight_codes[:, cols].bitcast(FP8X4),
                rhs_scale=weight_scales[:, cols],
                start=True,
                stop=True,
            )

        result_sb = sb.tile([P, PACK * Q], F32, name="result_sb")
        result_rows = result_sb[:].rearrange("p (t q) -> p t q", t=PACK)
        result_grouped = sb.tile([P, Q, PACK], BF16, name="result_grouped", align_bytes=MX_ALIGN)
        out_rows = out_0.rearrange("(p t) q -> p t q", t=PACK)

        early = ps.tile([P, 2, Q], F32, name="early", tag="scores0")
        for t in range(2):
            multiply(early[:, t, :], *quantize_values(t), slice(0, Q))
        nc.scalar.copy(result_rows[:, :2, :], early[:])
        nc.sync.dma_start(out_rows[:, :2, :], result_rows[:, :2, :])
        nc.vector.tensor_copy(result_grouped[:, :, :2], result_rows[:, :2, :].rearrange("p t q -> p q t"))

        halves = [slice(0, Q // 2), slice(Q // 2, Q)]
        late = [ps.tile([P, 2, Q // 2], F32, name="late%d" % h, tag=("scores1", "late1")[h]) for h in range(2)]
        for t in range(2, PACK):
            val_codes, val_scales = quantize_values(t)
            for h in range(2):
                multiply(late[h][:, t - 2, :], val_codes, val_scales, halves[h])
        for h, copy in enumerate((nc.vector.tensor_copy, nc.scalar.copy)):
            copy(result_grouped[:, halves[h], 2:], late[h][:].rearrange("p t q -> p q t"))
        for h in (1, 0):
            nc.scalar.copy(result_rows[:, 2:, halves[h]], late[h][:])
        nc.scalar.dma_start(out_rows[:, 2:, :], result_rows[:, 2:, :])

        result_codes = sb.tile([P, Q], U32, name="result_codes", align_bytes=MX_ALIGN)
        result_scales = sb.tile([P, Q], U8, name="result_scales", align_bytes=MX_ALIGN)
        nc.vector.quantize_mx(
            out=result_codes[:].bitcast(FP8X4), scales=result_scales[:], in_=result_grouped[:].rearrange("p q t -> p (q t)")
        )
        nc.sync.dma_start(out_1[0].rearrange("p q t -> p (q t)").bitcast(I32), result_codes[:].bitcast(I32))
        for quad in range(QUADRANTS):
            queue = nc.sync if quad < QUADRANTS // 2 else nc.scalar
            queue.dma_start(
                out_2[0, SCALE_ROWS * quad : SCALE_ROWS * (quad + 1), :].bitcast(I32),
                result_scales[32 * quad : 32 * quad + SCALE_ROWS, :].bitcast(I32),
            )
